import numpy as np
CORES = [2,10,118,126]
N = 4
def setup_inputs(rng):
    return {"x": rng.standard_normal((N, 128, 128), dtype=np.float32)}
def reference(x):
    g = np.concatenate(list(x), axis=1)
    return {"y": np.broadcast_to(g, (N,) + g.shape)}

@@ -1,0 +1,33 @@
+from concourse.bass import DstId, RemoteDMATransfer
+
+B = 128
+
+SCRATCH = {
+    "land": ("sbuf", [128, 4 * B], "float32"),
+}
+SEMAPHORES = ["loaded", "read", "arrived", "stored"]
+
+
+def rank_program(g, core, T, topo):
+    rank = T.rank_of(core)
+    if rank is None:
+        return
+    peers = [c for c in T.cores if c != core]
+    mine = T.land[:, rank * B:(rank + 1) * B]
+
+    g.sync.dma_start(mine, T.x[:]).then_inc(T.sem.loaded, 16)
+    g.wait_ge(T.sem.loaded, 16)
+
+    ids = []
+    for p in peers:
+        rid, pid, _se = topo.addr(p)
+        ids.append(DstId(rid=rid, pnc=pid))
+    g.remote_dma_fused(
+        [RemoteDMATransfer(dst_ids=ids, dma_engine_mask=0x00FF, remote_sem=T.sem.arrived,
+                           srcs=[mine], dsts=[mine for _p in peers])],
+        local_sem=T.sem.read)
+
+    g.wait_ge(T.sem.arrived, 8 * len(peers))
+    g.dma_start(T.y[:], T.land[:]).then_inc(T.sem.stored, 16)
+    g.wait_ge(T.sem.read, 8)
+    g.wait_ge(T.sem.stored, 16)

@@ -16,18 +16,20 @@ def rank_program(g, core, T, topo):
     mine = T.land[:, rank * B:(rank + 1) * B]
 
     g.sync.dma_start(mine, T.x[:]).then_inc(T.sem.loaded, 16)
-    g.wait_ge(T.sem.loaded, 16)
 
     ids = []
     for p in peers:
         rid, pid, _se = topo.addr(p)
         ids.append(DstId(rid=rid, pnc=pid))
+    g.wait_ge(T.sem.loaded, 16)
     g.remote_dma_fused(
         [RemoteDMATransfer(dst_ids=ids, dma_engine_mask=0x00FF, remote_sem=T.sem.arrived,
                            srcs=[mine], dsts=[mine for _p in peers])],
         local_sem=T.sem.read)
 
-    g.wait_ge(T.sem.arrived, 8 * len(peers))
-    g.dma_start(T.y[:], T.land[:]).then_inc(T.sem.stored, 16)
+    g.sync.wait_ge(T.sem.loaded, 16)
+    g.sync.wait_ge(T.sem.arrived, 8 * len(peers))
+    g.sync.dma_start(T.y[:], T.land[:]).then_inc(T.sem.stored, 16)
+
     g.wait_ge(T.sem.read, 8)
     g.wait_ge(T.sem.stored, 16)

from concourse.bass import DstId, RemoteDMATransfer

B = 128

SCRATCH = {
    "land": ("sbuf", [128, 4 * B], "float32"),
}
SEMAPHORES = ["loaded", "read", "arrived", "stored"]


def rank_program(g, core, T, topo):
    rank = T.rank_of(core)
    if rank is None:
        return
    peers = [c for c in T.cores if c != core]
    mine = T.land[:, rank * B:(rank + 1) * B]

    g.sync.dma_start(mine, T.x[:]).then_inc(T.sem.loaded, 16)

    ids = []
    for p in peers:
        rid, pid, _se = topo.addr(p)
        ids.append(DstId(rid=rid, pnc=pid))
    g.wait_ge(T.sem.loaded, 16)
    g.remote_dma_fused(
        [RemoteDMATransfer(dst_ids=ids, dma_engine_mask=0x00FF, remote_sem=T.sem.arrived,
                           srcs=[mine], dsts=[mine for _p in peers])],
        local_sem=T.sem.read)

    g.sync.wait_ge(T.sem.loaded, 16)
    g.sync.wait_ge(T.sem.arrived, 8 * len(peers))
    g.sync.dma_start(T.y[:], T.land[:]).then_inc(T.sem.stored, 16)

    g.wait_ge(T.sem.read, 8)
    g.wait_ge(T.sem.stored, 16)
